import numpy as np, ml_dtypes
CORES = [22,38,54,62,70,110,23,39,55,63,71,111]
N = 12
NH, QP = 12, 32
def setup_inputs(rng):
    return {"q": rng.standard_normal((N, 128, NH * QP), dtype=np.float32).astype(ml_dtypes.bfloat16), "k": rng.standard_normal((N, 128, NH * 128), dtype=np.float32).astype(ml_dtypes.bfloat16), "v": rng.standard_normal((N, 128, NH * 128), dtype=np.float32).astype(ml_dtypes.bfloat16)}
def setup_inputs_big(rng):
    d = setup_inputs(rng)
    for k in ("q", "k", "v"): d[k] = (d[k].astype(np.float32) * 1024.0).astype(d[k].dtype)
    return d
def setup_inputs_small(rng):
    d = setup_inputs(rng)
    for k in ("q", "k", "v"): d[k] = (d[k].astype(np.float32) * (1 / 1024.0)).astype(d[k].dtype)
    return d
def setup_inputs_apart(rng):
    d = setup_inputs(rng)
    f = (10.0 ** rng.permutation(np.linspace(-1.5, 1.5, N))).astype(np.float32).reshape(N, 1, 1)
    for k in ("q", "k", "v"): d[k] = (d[k].astype(np.float32) * f).astype(d[k].dtype)
    return d
def reference(q, k, v):
    Q, K, V = q.astype(np.float64), k.astype(np.float64), v.astype(np.float64)
    y = np.zeros((N, 128, NH * QP))
    for r in range(N):
        for h in range(NH):
            for j in range(N):
                S = np.maximum(K[j][:, 128 * h:128 * h + 128].T @ Q[r][:, QP * h:QP * h + QP], 0.0)
                y[r][:, QP * h:QP * h + QP] += V[j][:, 128 * h:128 * h + 128].T @ S
    return {"y": y.astype(ml_dtypes.bfloat16 if q.dtype != np.float64 else np.float64)}

@@ -1,0 +1,346 @@
+from concourse.bass import DstId, RemoteDMATransfer
+from concourse.mybir import AluOpType
+
+QP, KP = 32, 128
+BW = QP + 2 * KP
+WW = 2 * BW
+QQ = 2 * QP
+NC = 6
+
+CALLS = (((1, "D"),), ((0, "P"), (2, "D")), ((3, "D"),), ((4, "D"),), ((5, "D"),))
+NSTAY = 4
+PROC = (1, 0, 2, 3, 4, 5)
+CHUNKS = ((1,), (0, 2), (3, 4, 5))
+RETH = ()
+PAIRS = 8
+
+SEQ = tuple(s for call in CALLS for s, _ in call)
+HOW = {s: m for call in CALLS for s, m in call}
+RELAY = tuple(s for s in SEQ if HOW[s] == "R")
+
+
+def _steps():
+    def cut(lst):
+        n = -(-len(lst) // PAIRS)
+        return [lst[len(lst) * i // n:len(lst) * (i + 1) // n] for i in range(n)]
+    out = []
+    for t in range(NC):
+        old = [(t, pj, rw) for rw in range(t) for pj in (0, 1)]
+        new = [(wj, pj, t) for wj in range(t + 1) for pj in (0, 1)]
+        if t == NC - 1:
+            out += [cut(old), cut(new)]
+        else:
+            out.append(cut(old + new))
+    return out
+
+
+STEPS = _steps()
+NCHUNK = sum(len(st) for st in STEPS)
+NPAIR = sum(len(c) for st in STEPS for c in st)
+
+SCRATCH = {
+    "qs": ("sbuf", [128, 2 * NC * QP], "bfloat16"),
+    "ks": ("sbuf", [128, 2 * NC * KP], "bfloat16"),
+    "vs": ("sbuf", [128, 2 * NC * KP], "bfloat16"),
+    "stage": ("sbuf", [128, NC * WW], "bfloat16"),
+    "land": ("sbuf", [128, NC * WW], "bfloat16"),
+    "hbuf": ("sbuf", [128, 3 * WW], "bfloat16"),
+    "hob": ("sbuf", [128, NC * QQ], "bfloat16"),
+    "zero": ("sbuf", [128, PAIRS * QQ], "float32"),
+    "ssb": ("sbuf", [128, NPAIR * QQ], "bfloat16"),
+    "osb": ("sbuf", [128, NC * QQ], "bfloat16"),
+    "yl": ("sbuf", [128, 2 * NC * QP], "bfloat16"),
+    "sp0": ("psum", [128, 512], "float32"),
+    "sp1": ("psum", [128, 512], "float32"),
+}
+for _w in range(NC):
+    SCRATCH["op%d" % _w] = ("psum", [128, 512], "float32")
+
+SEMAPHORES = (["ldq", "zf", "selfp", "sent", "yarr", "own", "oca", "ocb", "stored", "hor"]
+              + ["ld%d" % i for i in range(len(CHUNKS))]
+              + ["pk%d" % i for i in range(len(CALLS))] + ["arr%d" % i for i in range(NC)]
+              + ["od%d" % i for i in range(NC)] + ["har%d" % i for i in range(3)]
+              + ["sd%d" % i for i in range(NCHUNK)] + ["rd%d" % i for i in range(NCHUNK)])
+
+_CACHE = {}
+
+
+def _perms(lst):
+    if len(lst) < 2:
+        return [list(lst)]
+    return [[x] + r for i, x in enumerate(lst) for r in _perms(lst[:i] + lst[i + 1:])]
+
+
+def _plan(T, topo):
+    if "p" in _CACHE:
+        return _CACHE["p"]
+    cores = list(T.cores)
+    chips = sorted({topo.chip(c) for c in cores})
+    every = range(max(chips) + 2)
+
+    def way(a, b):
+        if topo.same_plane(a, b):
+            return [("out", a), ("in", b)]
+        if topo.mates(a, b):
+            return [("mate", a)]
+        m = [x for x in every if topo.mates(a, x)][0]
+        return [("mate", a), ("out", m), ("in", b)]
+
+    best = None
+    for rest in _perms(chips[1:]):
+        ring = [chips[0]] + rest
+        load = {}
+        by_step = 0
+        for s in range(1, NC):
+            now = {}
+            for i, a in enumerate(ring):
+                for l in way(a, ring[(i + s) % NC]):
+                    key = (l, HOW[s])
+                    load[key] = load.get(key, 0) + 1
+                    now[key] = now.get(key, 0) + 1
+            by_step += max(now.values())
+        score = (max(load.values()), by_step, sum(v * v for v in load.values()))
+        if best is None or score < best[0]:
+            best = (score, ring)
+    ring = best[1]
+    mem = [sorted(c for c in cores if topo.chip(c) == ch) for ch in ring]
+    helper = {}
+    for two in mem:
+        cand = [x for x in range(max(cores) + 1)
+                if topo.chip(x) == topo.chip(two[0]) and x not in cores and topo.die(x) != topo.die(two[0])
+                and all(topo.may_write(x, d) for d in cores)]
+        for p, c in enumerate(two):
+            helper[c] = cand[p]
+    _CACHE["p"] = (mem, helper)
+    return _CACHE["p"]
+
+
+def _bits(m):
+    return [1 << e for e in range(m.bit_length()) if (m >> e) & 1]
+
+
+def _split(bits, n):
+    k = 1
+    while 2 * k * n <= len(bits):
+        k *= 2
+    return [sum(bits[i * k:(i + 1) * k]) for i in range(n)], k
+
+
+def _tr(topo, dst_core, mask, sem, src, dst):
+    rid, pid, _ = topo.addr(dst_core)
+    return RemoteDMATransfer(dst_ids=[DstId(rid=rid, pnc=pid)], dma_engine_mask=mask, remote_sem=sem, src=src, dst=dst)
+
+
+def _far(topo, core, mem):
+    return _bits(topo.mask(core, [two[0] for two in mem if topo.chip(two[0]) != topo.chip(core)][0]))
+
+
+def _wave(T, topo, mem, ci, p, s, masks, src_buf, src_base):
+    d = (ci + s) % NC
+    w = PROC.index(s)
+    return [_tr(topo, mem[d][pp], masks[pp], T.sem["arr%d" % w], src_buf[:, src_base + pp * BW:src_base + (pp + 1) * BW],
+                T.land[:, w * WW + p * BW:w * WW + (p + 1) * BW]) for pp in (0, 1)]
+
+
+def _ret(T, topo, mem, ci, p, waves, bits, src_buf, w0):
+    masks, k = _split(bits, 2 * len(waves))
+    head = 2 * ci + p
+    return [_tr(topo, mem[(ci - PROC[w]) % NC][pp], masks[2 * i + pp], T.sem.yarr,
+                src_buf[:, (w - w0) * QQ + pp * QP:(w - w0) * QQ + (pp + 1) * QP], T.yl[:, head * QP:(head + 1) * QP])
+            for i, w in enumerate(waves) for pp in (0, 1)], k
+
+
+def _helper(g, core, T, topo, mem, ci, p):
+    off = _far(topo, core, mem)
+    sent = 0
+    for k, s in enumerate(RELAY):
+        g.wait_ge(T.sem["har%d" % k], NSTAY)
+        masks, n = _split(off, 2)
+        g.remote_dma_fused(_wave(T, topo, mem, ci, p, s, masks, T.hbuf, k * WW), local_sem=T.sem.sent)
+        sent += 2 * n
+    if RETH:
+        g.wait_ge(T.sem.hor, NSTAY)
+        trs, n = _ret(T, topo, mem, ci, p, RETH, off, T.hob, RETH[0])
+        g.remote_dma_fused(trs, local_sem=T.sem.sent)
+        sent += n * len(trs)
+    g.wait_ge(T.sem.sent, sent)
+
+
+def rank_program(g, core, T, topo):
+    mem, helper = _plan(T, topo)
+    if RELAY or RETH:
+        for ci in range(NC):
+            for p in (0, 1):
+                if helper[mem[ci][p]] == core:
+                    _helper(g, core, T, topo, mem, ci, p)
+    if T.rank_of(core) is None:
+        return
+    ci = [i for i in range(NC) if core in mem[i]][0]
+    p = mem[ci].index(core)
+    head = 2 * ci + p
+    mate_core = mem[ci][1 - p]
+    sem = T.sem
+    ko, qo = (0, 2 * KP) if p == 0 else (QP, 0)
+    off = _far(topo, core, mem)
+    stay = [b for b in _bits(topo.mask(core, mate_core)) if b not in off][:NSTAY]
+
+    nld = []
+    for n, ch in enumerate(CHUNKS):
+        runs = []
+        for d in sorted((ci + s) % NC for s in ch):
+            if runs and runs[-1][1] == d:
+                runs[-1][1] = d + 1
+            else:
+                runs.append([d, d + 1])
+        for a, b in runs:
+            g.sync.dma_start(T.ks[:, 2 * a * KP:2 * b * KP], T.k[:, 2 * a * KP:2 * b * KP]).then_inc(sem["ld%d" % n], 16)
+            g.scalar.dma_start(T.vs[:, 2 * a * KP:2 * b * KP], T.v[:, 2 * a * KP:2 * b * KP]).then_inc(sem["ld%d" % n], 16)
+        nld.append(32 * len(runs))
+        if n == 0:
+            g.sync.dma_start(T.qs[:, :], T.q[:, :]).then_inc(sem.ldq, 16)
+
+    g.vector.memset(T.zero[:, :], 0.0).then_inc(sem.zf, 1)
+    seen = []
+    npk = []
+    for i, call in enumerate(CALLS):
+        npk.append(0)
+        for s, _ in call:
+            d = (ci + s) % NC
+            n = [x for x in range(len(CHUNKS)) if s in CHUNKS[x]][0]
+            if n not in seen:
+                g.vector.wait_ge(sem["ld%d" % n], nld[n])
+                if not seen:
+                    g.vector.wait_ge(sem.ldq, 16)
+                seen.append(n)
+            for pp in (0, 1):
+                h = 2 * d + pp
+                if s == 0 and pp == p:
+                    buf, base, done = T.land, PROC.index(0) * WW + p * BW, sem.selfp
+                else:
+                    buf, base, done = T.stage, d * WW + pp * BW, sem["pk%d" % i]
+                    npk[i] += 3
+                g.vector.tensor_copy(buf[:, base + ko:base + ko + KP], T.ks[:, h * KP:(h + 1) * KP]).then_inc(done, 1)
+                g.vector.tensor_copy(buf[:, base + ko + KP:base + ko + 2 * KP],
+                                     T.vs[:, h * KP:(h + 1) * KP]).then_inc(done, 1)
+                g.vector.tensor_copy(buf[:, base + qo:base + qo + QP], T.qs[:, h * QP:(h + 1) * QP]).then_inc(done, 1)
+
+    sent = 0
+    narr = {}
+    for i, call in enumerate(CALLS):
+        g.wait_ge(sem["pk%d" % i], npk[i])
+        fm, fk = _split(off, 2 * len([1 for _, m in call if m == "D"]) or 1)
+        nm, nk = _split(stay, len([1 for _, m in call if m == "P"]) + 2 * len([1 for _, m in call if m == "R"]) or 1)
+        trs = []
+        for s, m in call:
+            d = (ci + s) % NC
+            w = PROC.index(s)
+            if m == "D":
+                trs += _wave(T, topo, mem, ci, p, s, [fm.pop(0), fm.pop(0)], T.stage, d * WW)
+                sent += 2 * fk
+                narr[w] = 2 * fk
+            elif m == "P":
+                trs.append(_tr(topo, mate_core, nm.pop(0), sem["arr%d" % w],
+                               T.stage[:, d * WW + (1 - p) * BW:d * WW + (2 - p) * BW],
+                               T.land[:, w * WW + p * BW:w * WW + (p + 1) * BW]))
+                sent += nk
+                narr[w] = nk
+            else:
+                k = RELAY.index(s)
+                for pp in (0, 1):
+                    trs.append(_tr(topo, helper[core], nm.pop(0), sem["har%d" % k],
+                                   T.stage[:, d * WW + pp * BW:d * WW + (pp + 1) * BW],
+                                   T.hbuf[:, k * WW + pp * BW:k * WW + (pp + 1) * BW]))
+                sent += 2 * nk
+                narr[w] = 2 * _split(off, 2)[1]
+        g.remote_dma_fused(trs, local_sem=sem.sent)
+
+    sp = [T.sp0, T.sp1]
+    nacc = [0] * NC
+    cid = [0]
+    col = [0]
+    waited = []
+
+    def kv(wj, pj):
+        base = wj * WW + pj * BW + (0 if pj == 0 else QP)
+        return base, base + KP
+
+    def emit_s(chunk):
+        c = cid[0]
+        cid[0] += 1
+        bank = sp[c % 2]
+        for x, (wj, pj, rw) in enumerate(chunk):
+            kb = kv(wj, pj)[0]
+            g.tensor.matmul(bank[:, x * QQ:(x + 1) * QQ], T.land[:, kb:kb + KP],
+                            T.land[:, rw * WW + 2 * KP:rw * WW + 2 * KP + QQ], True, True).then_inc(sem["sd%d" % c], 1)
+        n = len(chunk) * QQ
+        g.vector.wait_ge(sem["sd%d" % c], len(chunk))
+        g.vector.tensor_tensor(T.ssb[:, col[0]:col[0] + n], bank[:, 0:n], T.zero[:, 0:n],
+                               AluOpType.max).then_inc(sem["rd%d" % c], 1)
+        col[0] += n
+        return c, col[0] - n
+
+    def emit_o(chunk, c, base):
+        g.tensor.wait_ge(sem["rd%d" % c], 1)
+        for x, (wj, pj, rw) in enumerate(chunk):
+            vb = kv(wj, pj)[1]
+            g.tensor.matmul(T["op%d" % rw][:, 0:QQ], T.land[:, vb:vb + KP], T.ssb[:, base + x * QQ:base + (x + 1) * QQ],
+                            nacc[rw] == 0, nacc[rw] == 2 * NC - 1).then_inc(sem["od%d" % rw], 1)
+            nacc[rw] += 1
+
+    def copy_out(w, done):
+        g.vector.wait_ge(sem["od%d" % w], 2 * NC)
+        if PROC[w] == 0:
+            g.vector.tensor_copy(T.yl[:, head * QP:(head + 1) * QP],
+                                 T["op%d" % w][:, p * QP:(p + 1) * QP]).then_inc(sem.own, 1)
+            q = 1 - p
+            g.vector.tensor_copy(T.osb[:, w * QQ + q * QP:w * QQ + (q + 1) * QP],
+                                 T["op%d" % w][:, q * QP:(q + 1) * QP]).then_inc(done, 1)
+        else:
+            g.vector.tensor_copy(T.osb[:, w * QQ:(w + 1) * QQ], T["op%d" % w][:, 0:QQ]).then_inc(done, 1)
+
+    g.vector.wait_ge(sem.zf, 1)
+    for si, st in enumerate(STEPS):
+        t = min(si, NC - 1)
+        if t not in waited:
+            waited.append(t)
+            g.tensor.wait_ge(sem["arr%d" % t], narr[t])
+            if PROC[t] == 0:
+                g.tensor.wait_ge(sem.selfp, 3)
+        prev = None
+        for chunk in st:
+            cur = (chunk,) + emit_s(chunk)
+            if prev:
+                emit_o(*prev)
+            prev = cur
+        emit_o(*prev)
+        if si == NC - 1:
+            for w in range(NC - 1):
+                copy_out(w, sem.oca)
+    copy_out(NC - 1, sem.ocb)
+
+    g.wait_ge(sem.oca, NC - 1)
+    nyarr = 0
+    if RETH:
+        rid, pid, _ = topo.addr(helper[core])
+        g.remote_dma(T.hob[:, 0:len(RETH) * QQ], T.osb[:, RETH[0] * QQ:(RETH[-1] + 1) * QQ], sem.hor, sem.sent, pid, rid,
+                     sum(stay))
+        sent += len(stay)
+        nyarr += 2 * len(RETH) * _split(off, 2 * len(RETH))[1]
+    w0 = PROC.index(0)
+    trs, k = _ret(T, topo, mem, ci, p, [w for w in range(NC - 1) if w != w0 and w not in RETH], off, T.osb, 0)
+    sent += k * len(trs) + len(stay)
+    nyarr += k * len(trs) + len(stay)
+    trs.append(_tr(topo, mate_core, sum(stay), sem.yarr, T.osb[:, w0 * QQ + (1 - p) * QP:w0 * QQ + (2 - p) * QP],
+                   T.yl[:, head * QP:(head + 1) * QP]))
+    g.remote_dma_fused(trs, local_sem=sem.sent)
+    g.wait_ge(sem.ocb, 1)
+    trs, k = _ret(T, topo, mem, ci, p, [NC - 1], off, T.osb, 0)
+    g.remote_dma_fused(trs, local_sem=sem.sent)
+    sent += k * len(trs)
+    nyarr += k * len(trs)
+    g.wait_ge(sem.sent, sent)
+
+    g.sync.wait_ge(sem.yarr, nyarr)
+    g.sync.wait_ge(sem.own, 1)
+    g.sync.dma_start(T.y[:, :], T.yl[:, :]).then_inc(sem.stored, 16)
+    g.sync.wait_ge(sem.stored, 16)

@@ -7,10 +7,10 @@ WW = 2 * BW
 QQ = 2 * QP
 NC = 6
 
-CALLS = (((1, "D"),), ((0, "P"), (2, "D")), ((3, "D"),), ((4, "D"),), ((5, "D"),))
-NSTAY = 4
-PROC = (1, 0, 2, 3, 4, 5)
-CHUNKS = ((1,), (0, 2), (3, 4, 5))
+CALLS = (((1, "R"),), ((2, "D"),), ((3, "R"), (4, "D")), ((5, "D"),), ((0, "P"),))
+NSTAY = 8
+PROC = (2, 0, 4, 1, 5, 3)
+CHUNKS = ((1,), (2,), (3, 4), (5, 0))
 RETH = ()
 PAIRS = 8
 
@@ -185,6 +185,7 @@ def rank_program(g, core, T, topo):
     stay = [b for b in _bits(topo.mask(core, mate_core)) if b not in off][:NSTAY]
 
     nld = []
+    g.sync.dma_start(T.qs[:, :], T.q[:, :]).then_inc(sem.ldq, 16)
     for n, ch in enumerate(CHUNKS):
         runs = []
         for d in sorted((ci + s) % NC for s in ch):
@@ -196,40 +197,49 @@ def rank_program(g, core, T, topo):
             g.sync.dma_start(T.ks[:, 2 * a * KP:2 * b * KP], T.k[:, 2 * a * KP:2 * b * KP]).then_inc(sem["ld%d" % n], 16)
             g.scalar.dma_start(T.vs[:, 2 * a * KP:2 * b * KP], T.v[:, 2 * a * KP:2 * b * KP]).then_inc(sem["ld%d" % n], 16)
         nld.append(32 * len(runs))
-        if n == 0:
-            g.sync.dma_start(T.qs[:, :], T.q[:, :]).then_inc(sem.ldq, 16)
+    n0 = [x for x in range(len(CHUNKS)) if 0 in CHUNKS[x]][0]
+    w0 = PROC.index(0)
+    mine = w0 * WW + p * BW
 
     g.vector.memset(T.zero[:, :], 0.0).then_inc(sem.zf, 1)
     seen = []
     npk = []
+    g.vector.wait_ge(sem.ldq, 16)
     for i, call in enumerate(CALLS):
         npk.append(0)
         for s, _ in call:
             d = (ci + s) % NC
+            if s == 0:
+                g.vector.tensor_copy(T.land[:, mine + qo:mine + qo + QP],
+                                     T.qs[:, head * QP:(head + 1) * QP]).then_inc(sem.selfp, 1)
+                continue
             n = [x for x in range(len(CHUNKS)) if s in CHUNKS[x]][0]
             if n not in seen:
                 g.vector.wait_ge(sem["ld%d" % n], nld[n])
-                if not seen:
-                    g.vector.wait_ge(sem.ldq, 16)
                 seen.append(n)
             for pp in (0, 1):
                 h = 2 * d + pp
-                if s == 0 and pp == p:
-                    buf, base, done = T.land, PROC.index(0) * WW + p * BW, sem.selfp
-                else:
-                    buf, base, done = T.stage, d * WW + pp * BW, sem["pk%d" % i]
-                    npk[i] += 3
-                g.vector.tensor_copy(buf[:, base + ko:base + ko + KP], T.ks[:, h * KP:(h + 1) * KP]).then_inc(done, 1)
-                g.vector.tensor_copy(buf[:, base + ko + KP:base + ko + 2 * KP],
+                base, done = d * WW + pp * BW, sem["pk%d" % i]
+                npk[i] += 3
+                g.vector.tensor_copy(T.stage[:, base + ko:base + ko + KP], T.ks[:, h * KP:(h + 1) * KP]).then_inc(done, 1)
+                g.vector.tensor_copy(T.stage[:, base + ko + KP:base + ko + 2 * KP],
                                      T.vs[:, h * KP:(h + 1) * KP]).then_inc(done, 1)
-                g.vector.tensor_copy(buf[:, base + qo:base + qo + QP], T.qs[:, h * QP:(h + 1) * QP]).then_inc(done, 1)
+                g.vector.tensor_copy(T.stage[:, base + qo:base + qo + QP], T.qs[:, h * QP:(h + 1) * QP]).then_inc(done, 1)
 
-    sent = 0
-    narr = {}
+    sent = len(stay)
+    narr = {w0: len(stay)}
+    hn = 2 * ci + 1 - p
+    rid, pid, _ = topo.addr(mate_core)
+    g.wait_ge(sem.ldq, 16)
+    g.remote_dma(T.land[:, mine + qo:mine + qo + QP], T.qs[:, hn * QP:(hn + 1) * QP], sem["arr%d" % w0], sem.sent, pid, rid,
+                 sum(stay))
     for i, call in enumerate(CALLS):
-        g.wait_ge(sem["pk%d" % i], npk[i])
+        if npk[i]:
+            g.wait_ge(sem["pk%d" % i], npk[i])
+        else:
+            g.wait_ge(sem["ld%d" % n0], nld[n0])
         fm, fk = _split(off, 2 * len([1 for _, m in call if m == "D"]) or 1)
-        nm, nk = _split(stay, len([1 for _, m in call if m == "P"]) + 2 * len([1 for _, m in call if m == "R"]) or 1)
+        nm, nk = _split(stay, 2 * len([1 for _, m in call if m != "D"]) or 1)
         trs = []
         for s, m in call:
             d = (ci + s) % NC
@@ -239,11 +249,11 @@ def rank_program(g, core, T, topo):
                 sent += 2 * fk
                 narr[w] = 2 * fk
             elif m == "P":
-                trs.append(_tr(topo, mate_core, nm.pop(0), sem["arr%d" % w],
-                               T.stage[:, d * WW + (1 - p) * BW:d * WW + (2 - p) * BW],
-                               T.land[:, w * WW + p * BW:w * WW + (p + 1) * BW]))
-                sent += nk
-                narr[w] = nk
+                for x, buf in enumerate((T.ks, T.vs)):
+                    trs.append(_tr(topo, mate_core, nm.pop(0), sem["arr%d" % w], buf[:, hn * KP:(hn + 1) * KP],
+                                   T.land[:, mine + ko + x * KP:mine + ko + (x + 1) * KP]))
+                sent += 2 * nk
+                narr[w] += 2 * nk
             else:
                 k = RELAY.index(s)
                 for pp in (0, 1):
@@ -261,16 +271,17 @@ def rank_program(g, core, T, topo):
     waited = []
 
     def kv(wj, pj):
+        if wj == w0 and pj == p:
+            return T.ks[:, head * KP:(head + 1) * KP], T.vs[:, head * KP:(head + 1) * KP]
         base = wj * WW + pj * BW + (0 if pj == 0 else QP)
-        return base, base + KP
+        return T.land[:, base:base + KP], T.land[:, base + KP:base + 2 * KP]
 
     def emit_s(chunk):
         c = cid[0]
         cid[0] += 1
         bank = sp[c % 2]
         for x, (wj, pj, rw) in enumerate(chunk):
-            kb = kv(wj, pj)[0]
-            g.tensor.matmul(bank[:, x * QQ:(x + 1) * QQ], T.land[:, kb:kb + KP],
+            g.tensor.matmul(bank[:, x * QQ:(x + 1) * QQ], kv(wj, pj)[0],
                             T.land[:, rw * WW + 2 * KP:rw * WW + 2 * KP + QQ], True, True).then_inc(sem["sd%d" % c], 1)
         n = len(chunk) * QQ
         g.vector.wait_ge(sem["sd%d" % c], len(chunk))
@@ -282,8 +293,7 @@ def rank_program(g, core, T, topo):
     def emit_o(chunk, c, base):
         g.tensor.wait_ge(sem["rd%d" % c], 1)
         for x, (wj, pj, rw) in enumerate(chunk):
-            vb = kv(wj, pj)[1]
-            g.tensor.matmul(T["op%d" % rw][:, 0:QQ], T.land[:, vb:vb + KP], T.ssb[:, base + x * QQ:base + (x + 1) * QQ],
+            g.tensor.matmul(T["op%d" % rw][:, 0:QQ], kv(wj, pj)[1], T.ssb[:, base + x * QQ:base + (x + 1) * QQ],
                             nacc[rw] == 0, nacc[rw] == 2 * NC - 1).then_inc(sem["od%d" % rw], 1)
             nacc[rw] += 1
 
@@ -305,7 +315,8 @@ def rank_program(g, core, T, topo):
             waited.append(t)
             g.tensor.wait_ge(sem["arr%d" % t], narr[t])
             if PROC[t] == 0:
-                g.tensor.wait_ge(sem.selfp, 3)
+                g.tensor.wait_ge(sem.selfp, 1)
+                g.tensor.wait_ge(sem["ld%d" % n0], nld[n0])
         prev = None
         for chunk in st:
             cur = (chunk,) + emit_s(chunk)
@@ -326,7 +337,6 @@ def rank_program(g, core, T, topo):
                      sum(stay))
         sent += len(stay)
         nyarr += 2 * len(RETH) * _split(off, 2 * len(RETH))[1]
-    w0 = PROC.index(0)
     trs, k = _ret(T, topo, mem, ci, p, [w for w in range(NC - 1) if w != w0 and w not in RETH], off, T.osb, 0)
     sent += k * len(trs) + len(stay)
     nyarr += k * len(trs) + len(stay)

@@ -2,65 +2,44 @@ from concourse.bass import DstId, RemoteDMATransfer
 from concourse.mybir import AluOpType
 
 QP, KP = 32, 128
-BW = QP + 2 * KP
-WW = 2 * BW
-QQ = 2 * QP
 NC = 6
-
-CALLS = (((1, "R"),), ((2, "D"),), ((3, "R"), (4, "D")), ((5, "D"),), ((0, "P"),))
-NSTAY = 8
-PROC = (2, 0, 4, 1, 5, 3)
-CHUNKS = ((1,), (2,), (3, 4), (5, 0))
-RETH = ()
-PAIRS = 8
-
-SEQ = tuple(s for call in CALLS for s, _ in call)
-HOW = {s: m for call in CALLS for s, m in call}
-RELAY = tuple(s for s in SEQ if HOW[s] == "R")
-
-
-def _steps():
-    def cut(lst):
-        n = -(-len(lst) // PAIRS)
-        return [lst[len(lst) * i // n:len(lst) * (i + 1) // n] for i in range(n)]
-    out = []
-    for t in range(NC):
-        old = [(t, pj, rw) for rw in range(t) for pj in (0, 1)]
-        new = [(wj, pj, t) for wj in range(t + 1) for pj in (0, 1)]
-        if t == NC - 1:
-            out += [cut(old), cut(new)]
-        else:
-            out.append(cut(old + new))
-    return out
-
-
-STEPS = _steps()
-NCHUNK = sum(len(st) for st in STEPS)
-NPAIR = sum(len(c) for st in STEPS for c in st)
+HW = 3
+QQ = 2 * QP
+QS = HW * QP
+QB = 2 * QS
+KS = HW * KP
+YW = 12 * QP
+SW = 2 * HW * QQ
+QCALLS = ((1, 2), (3, 4), (5,))
+RCALLS = ((0,), (1, 2), (3, 4), (5,))
+NOP = 4
 
 SCRATCH = {
-    "qs": ("sbuf", [128, 2 * NC * QP], "bfloat16"),
-    "ks": ("sbuf", [128, 2 * NC * KP], "bfloat16"),
-    "vs": ("sbuf", [128, 2 * NC * KP], "bfloat16"),
-    "stage": ("sbuf", [128, NC * WW], "bfloat16"),
-    "land": ("sbuf", [128, NC * WW], "bfloat16"),
-    "hbuf": ("sbuf", [128, 3 * WW], "bfloat16"),
-    "hob": ("sbuf", [128, NC * QQ], "bfloat16"),
-    "zero": ("sbuf", [128, PAIRS * QQ], "float32"),
-    "ssb": ("sbuf", [128, NPAIR * QQ], "bfloat16"),
-    "osb": ("sbuf", [128, NC * QQ], "bfloat16"),
-    "yl": ("sbuf", [128, 2 * NC * QP], "bfloat16"),
+    "qs": ("sbuf", [128, 12 * QP], "bfloat16"),
+    "ks": ("sbuf", [128, 12 * KP], "bfloat16"),
+    "vs": ("sbuf", [128, 12 * KP], "bfloat16"),
+    "qraw": ("sbuf", [128, QB], "bfloat16"),
+    "qall": ("sbuf", [128, NC * QB], "bfloat16"),
+    "kl": ("sbuf", [128, 2 * KS], "bfloat16"),
+    "vl": ("sbuf", [128, 2 * KS], "bfloat16"),
+    "zero": ("sbuf", [128, SW], "float32"),
+    "ones": ("sbuf", [128, 128], "bfloat16"),
+    "ident": ("sbuf", [128, 128], "bfloat16"),
+    "ssb": ("sbuf", [128, NC * SW], "bfloat16"),
+    "osb": ("sbuf", [128, NC * QB], "bfloat16"),
+    "yl": ("sbuf", [128, NC * YW], "bfloat16"),
+    "yo": ("sbuf", [128, YW], "bfloat16"),
     "sp0": ("psum", [128, 512], "float32"),
     "sp1": ("psum", [128, 512], "float32"),
+    "ysum": ("psum", [128, 512], "float32"),
 }
-for _w in range(NC):
+for _w in range(NOP):
     SCRATCH["op%d" % _w] = ("psum", [128, 512], "float32")
 
-SEMAPHORES = (["ldq", "zf", "selfp", "sent", "yarr", "own", "oca", "ocb", "stored", "hor"]
-              + ["ld%d" % i for i in range(len(CHUNKS))]
-              + ["pk%d" % i for i in range(len(CALLS))] + ["arr%d" % i for i in range(NC)]
-              + ["od%d" % i for i in range(NC)] + ["har%d" % i for i in range(3)]
-              + ["sd%d" % i for i in range(NCHUNK)] + ["rd%d" % i for i in range(NCHUNK)])
+SEMAPHORES = (["ldq", "ldh", "ldn", "ldo", "zf", "onesf", "idn", "qh", "pk", "kva", "sent", "ysd", "yc", "stored"]
+              + ["arrq%d" % i for i in range(NC)] + ["ya%d" % i for i in range(NC)]
+              + ["sd%d" % i for i in range(NC)] + ["rd%d" % i for i in range(NC)]
+              + ["od%d" % i for i in range(NC)] + ["oc%d" % i for i in range(NC)])
 
 _CACHE = {}
 
@@ -89,29 +68,27 @@ def _plan(T, topo):
     best = None
     for rest in _perms(chips[1:]):
         ring = [chips[0]] + rest
-        load = {}
         by_step = 0
+        sq = 0
         for s in range(1, NC):
             now = {}
             for i, a in enumerate(ring):
                 for l in way(a, ring[(i + s) % NC]):
-                    key = (l, HOW[s])
-                    load[key] = load.get(key, 0) + 1
-                    now[key] = now.get(key, 0) + 1
+                    now[l] = now.get(l, 0) + 1
             by_step += max(now.values())
-        score = (max(load.values()), by_step, sum(v * v for v in load.values()))
+            sq += sum(v * v for v in now.values())
+        score = (by_step, sq)
         if best is None or score < best[0]:
             best = (score, ring)
     ring = best[1]
     mem = [sorted(c for c in cores if topo.chip(c) == ch) for ch in ring]
-    helper = {}
+    work = []
     for two in mem:
         cand = [x for x in range(max(cores) + 1)
                 if topo.chip(x) == topo.chip(two[0]) and x not in cores and topo.die(x) != topo.die(two[0])
                 and all(topo.may_write(x, d) for d in cores)]
-        for p, c in enumerate(two):
-            helper[c] = cand[p]
-    _CACHE["p"] = (mem, helper)
+        work.append(list(two) + cand[:2])
+    _CACHE["p"] = (mem, work)
     return _CACHE["p"]
 
 
@@ -131,226 +108,153 @@ def _tr(topo, dst_core, mask, sem, src, dst):
     return RemoteDMATransfer(dst_ids=[DstId(rid=rid, pnc=pid)], dma_engine_mask=mask, remote_sem=sem, src=src, dst=dst)
 
 
-def _far(topo, core, mem):
-    return _bits(topo.mask(core, [two[0] for two in mem if topo.chip(two[0]) != topo.chip(core)][0]))
-
-
-def _wave(T, topo, mem, ci, p, s, masks, src_buf, src_base):
-    d = (ci + s) % NC
-    w = PROC.index(s)
-    return [_tr(topo, mem[d][pp], masks[pp], T.sem["arr%d" % w], src_buf[:, src_base + pp * BW:src_base + (pp + 1) * BW],
-                T.land[:, w * WW + p * BW:w * WW + (p + 1) * BW]) for pp in (0, 1)]
-
-
-def _ret(T, topo, mem, ci, p, waves, bits, src_buf, w0):
-    masks, k = _split(bits, 2 * len(waves))
-    head = 2 * ci + p
-    return [_tr(topo, mem[(ci - PROC[w]) % NC][pp], masks[2 * i + pp], T.sem.yarr,
-                src_buf[:, (w - w0) * QQ + pp * QP:(w - w0) * QQ + (pp + 1) * QP], T.yl[:, head * QP:(head + 1) * QP])
-            for i, w in enumerate(waves) for pp in (0, 1)], k
-
-
-def _helper(g, core, T, topo, mem, ci, p):
-    off = _far(topo, core, mem)
-    sent = 0
-    for k, s in enumerate(RELAY):
-        g.wait_ge(T.sem["har%d" % k], NSTAY)
-        masks, n = _split(off, 2)
-        g.remote_dma_fused(_wave(T, topo, mem, ci, p, s, masks, T.hbuf, k * WW), local_sem=T.sem.sent)
-        sent += 2 * n
-    if RETH:
-        g.wait_ge(T.sem.hor, NSTAY)
-        trs, n = _ret(T, topo, mem, ci, p, RETH, off, T.hob, RETH[0])
-        g.remote_dma_fused(trs, local_sem=T.sem.sent)
-        sent += n * len(trs)
-    g.wait_ge(T.sem.sent, sent)
-
-
 def rank_program(g, core, T, topo):
-    mem, helper = _plan(T, topo)
-    if RELAY or RETH:
-        for ci in range(NC):
-            for p in (0, 1):
-                if helper[mem[ci][p]] == core:
-                    _helper(g, core, T, topo, mem, ci, p)
-    if T.rank_of(core) is None:
+    mem, work = _plan(T, topo)
+    here = [(i, four.index(core)) for i, four in enumerate(work) if core in four]
+    if not here:
         return
-    ci = [i for i in range(NC) if core in mem[i]][0]
-    p = mem[ci].index(core)
-    head = 2 * ci + p
-    mate_core = mem[ci][1 - p]
+    ci, w = here[0]
+    rank = w < 2
     sem = T.sem
-    ko, qo = (0, 2 * KP) if p == 0 else (QP, 0)
-    off = _far(topo, core, mem)
-    stay = [b for b in _bits(topo.mask(core, mate_core)) if b not in off][:NSTAY]
+    off = _bits(topo.mask(core, work[(ci + 1) % NC][w]))
+    stay = [b for b in _bits(topo.mask(core, work[ci][(w + 1) % 4])) if b not in off]
+    qhe = _split(off, 3)[1]
+    khe = _split(stay, 4)[1]
+    kne = _split(stay, 2)[1]
+    sent = 0
 
-    nld = []
-    g.sync.dma_start(T.qs[:, :], T.q[:, :]).then_inc(sem.ldq, 16)
-    for n, ch in enumerate(CHUNKS):
-        runs = []
-        for d in sorted((ci + s) % NC for s in ch):
-            if runs and runs[-1][1] == d:
-                runs[-1][1] = d + 1
-            else:
-                runs.append([d, d + 1])
-        for a, b in runs:
-            g.sync.dma_start(T.ks[:, 2 * a * KP:2 * b * KP], T.k[:, 2 * a * KP:2 * b * KP]).then_inc(sem["ld%d" % n], 16)
-            g.scalar.dma_start(T.vs[:, 2 * a * KP:2 * b * KP], T.v[:, 2 * a * KP:2 * b * KP]).then_inc(sem["ld%d" % n], 16)
-        nld.append(32 * len(runs))
-    n0 = [x for x in range(len(CHUNKS)) if 0 in CHUNKS[x]][0]
-    w0 = PROC.index(0)
-    mine = w0 * WW + p * BW
+    if rank:
+        g.sync.dma_start(T.qs[:, :], T.q[:, :]).then_inc(sem.ldq, 16)
+        for a, b, s in ((2 * KS, 4 * KS, sem.ldh), ((1 - w) * KS, (2 - w) * KS, sem.ldn), (w * KS, (w + 1) * KS, sem.ldo)):
+            g.sync.dma_start(T.ks[:, a:b], T.k[:, a:b]).then_inc(s, 16)
+            g.scalar.dma_start(T.vs[:, a:b], T.v[:, a:b]).then_inc(s, 16)
 
     g.vector.memset(T.zero[:, :], 0.0).then_inc(sem.zf, 1)
-    seen = []
-    npk = []
-    g.vector.wait_ge(sem.ldq, 16)
-    for i, call in enumerate(CALLS):
-        npk.append(0)
-        for s, _ in call:
-            d = (ci + s) % NC
-            if s == 0:
-                g.vector.tensor_copy(T.land[:, mine + qo:mine + qo + QP],
-                                     T.qs[:, head * QP:(head + 1) * QP]).then_inc(sem.selfp, 1)
-                continue
-            n = [x for x in range(len(CHUNKS)) if s in CHUNKS[x]][0]
-            if n not in seen:
-                g.vector.wait_ge(sem["ld%d" % n], nld[n])
-                seen.append(n)
-            for pp in (0, 1):
-                h = 2 * d + pp
-                base, done = d * WW + pp * BW, sem["pk%d" % i]
-                npk[i] += 3
-                g.vector.tensor_copy(T.stage[:, base + ko:base + ko + KP], T.ks[:, h * KP:(h + 1) * KP]).then_inc(done, 1)
-                g.vector.tensor_copy(T.stage[:, base + ko + KP:base + ko + 2 * KP],
-                                     T.vs[:, h * KP:(h + 1) * KP]).then_inc(done, 1)
-                g.vector.tensor_copy(T.stage[:, base + qo:base + qo + QP], T.qs[:, h * QP:(h + 1) * QP]).then_inc(done, 1)
-
-    sent = len(stay)
-    narr = {w0: len(stay)}
-    hn = 2 * ci + 1 - p
-    rid, pid, _ = topo.addr(mate_core)
-    g.wait_ge(sem.ldq, 16)
-    g.remote_dma(T.land[:, mine + qo:mine + qo + QP], T.qs[:, hn * QP:(hn + 1) * QP], sem["arr%d" % w0], sem.sent, pid, rid,
-                 sum(stay))
-    for i, call in enumerate(CALLS):
-        if npk[i]:
-            g.wait_ge(sem["pk%d" % i], npk[i])
-        else:
-            g.wait_ge(sem["ld%d" % n0], nld[n0])
-        fm, fk = _split(off, 2 * len([1 for _, m in call if m == "D"]) or 1)
-        nm, nk = _split(stay, 2 * len([1 for _, m in call if m != "D"]) or 1)
-        trs = []
-        for s, m in call:
-            d = (ci + s) % NC
-            w = PROC.index(s)
-            if m == "D":
-                trs += _wave(T, topo, mem, ci, p, s, [fm.pop(0), fm.pop(0)], T.stage, d * WW)
-                sent += 2 * fk
-                narr[w] = 2 * fk
-            elif m == "P":
-                for x, buf in enumerate((T.ks, T.vs)):
-                    trs.append(_tr(topo, mate_core, nm.pop(0), sem["arr%d" % w], buf[:, hn * KP:(hn + 1) * KP],
-                                   T.land[:, mine + ko + x * KP:mine + ko + (x + 1) * KP]))
-                sent += 2 * nk
-                narr[w] += 2 * nk
+    if rank:
+        g.vector.memset(T.ones[:, :], 1.0).then_inc(sem.onesf, 1)
+        g.vector.wait_ge(sem.ldq, 16)
+    g.vector.wait_ge(sem.qh, qhe * (1 if rank else 2))
+    for a in range(HW):
+        for pp in (0, 1):
+            if rank and pp == w:
+                src = T.qs[:, (w * HW + a) * QP:(w * HW + a + 1) * QP]
             else:
-                k = RELAY.index(s)
-                for pp in (0, 1):
-                    trs.append(_tr(topo, helper[core], nm.pop(0), sem["har%d" % k],
-                                   T.stage[:, d * WW + pp * BW:d * WW + (pp + 1) * BW],
-                                   T.hbuf[:, k * WW + pp * BW:k * WW + (pp + 1) * BW]))
-                sent += 2 * nk
-                narr[w] = 2 * _split(off, 2)[1]
+                src = T.qraw[:, pp * QS + a * QP:pp * QS + (a + 1) * QP]
+            g.vector.tensor_copy(T.qall[:, a * QQ + pp * QP:a * QQ + (pp + 1) * QP], src).then_inc(sem.pk, 1)
+    g.vector.wait_ge(sem.zf, 1)
+
+    if rank:
+        g.wait_ge(sem.onesf, 1)
+        g.affine_select(T.ident[:, :], T.ones[:, :], [[-1, 128]], AluOpType.is_equal, 0.0, 0, 1).then_inc(sem.idn, 1)
+        g.wait_ge(sem.ldq, 16)
+        m, k = _split(off, 3)
+        g.remote_dma_fused([_tr(topo, work[ci][x], m[i], sem.qh, T.qs[:, x * QS:(x + 1) * QS], T.qraw[:, w * QS:(w + 1) * QS])
+                            for i, x in enumerate(y for y in range(4) if y != w)], local_sem=sem.sent)
+        sent += 3 * k
+        g.wait_ge(sem.ldh, 32)
+        m, k = _split(stay, 4)
+        trs = []
+        for x in (2, 3):
+            for src, dst in ((T.ks, T.kl), (T.vs, T.vl)):
+                trs.append(_tr(topo, work[ci][x], m.pop(0), sem.kva, src[:, x * KS:(x + 1) * KS], dst[:, w * KS:(w + 1) * KS]))
         g.remote_dma_fused(trs, local_sem=sem.sent)
+        sent += 4 * k
+        g.wait_ge(sem.ldn, 32)
+        m, k = _split(stay, 2)
+        x = 1 - w
+        g.remote_dma_fused([_tr(topo, work[ci][x], m[i], sem.kva, src[:, x * KS:(x + 1) * KS], dst[:, w * KS:(w + 1) * KS])
+                            for i, (src, dst) in enumerate(((T.ks, T.kl), (T.vs, T.vl)))], local_sem=sem.sent)
+        sent += 2 * k
+
+    narr = {}
+    g.wait_ge(sem.pk, 2 * HW)
+    for call in QCALLS:
+        m, k = _split(off, len(call))
+        g.remote_dma_fused([_tr(topo, work[(ci + s) % NC][w], m[i], sem["arrq%d" % s], T.qall[:, 0:QB],
+                                T.qall[:, s * QB:(s + 1) * QB]) for i, s in enumerate(call)], local_sem=sem.sent)
+        sent += k * len(call)
+        for s in call:
+            narr[s] = k
 
     sp = [T.sp0, T.sp1]
-    nacc = [0] * NC
-    cid = [0]
-    col = [0]
-    waited = []
 
-    def kv(wj, pj):
-        if wj == w0 and pj == p:
-            return T.ks[:, head * KP:(head + 1) * KP], T.vs[:, head * KP:(head + 1) * KP]
-        base = wj * WW + pj * BW + (0 if pj == 0 else QP)
-        return T.land[:, base:base + KP], T.land[:, base + KP:base + 2 * KP]
+    def kv(kb, a):
+        if rank and kb == w:
+            c = (w * HW + a) * KP
+            return T.ks[:, c:c + KP], T.vs[:, c:c + KP]
+        c = kb * KS + a * KP
+        return T.kl[:, c:c + KP], T.vl[:, c:c + KP]
 
-    def emit_s(chunk):
-        c = cid[0]
-        cid[0] += 1
-        bank = sp[c % 2]
-        for x, (wj, pj, rw) in enumerate(chunk):
-            g.tensor.matmul(bank[:, x * QQ:(x + 1) * QQ], kv(wj, pj)[0],
-                            T.land[:, rw * WW + 2 * KP:rw * WW + 2 * KP + QQ], True, True).then_inc(sem["sd%d" % c], 1)
-        n = len(chunk) * QQ
-        g.vector.wait_ge(sem["sd%d" % c], len(chunk))
-        g.vector.tensor_tensor(T.ssb[:, col[0]:col[0] + n], bank[:, 0:n], T.zero[:, 0:n],
-                               AluOpType.max).then_inc(sem["rd%d" % c], 1)
-        col[0] += n
-        return c, col[0] - n
+    def emit_s(t):
+        if t:
+            g.tensor.wait_ge(sem["arrq%d" % t], narr[t])
+        bank = sp[t % 2]
+        for a in range(HW):
+            for kb in (0, 1):
+                x = 2 * a + kb
+                g.tensor.matmul(bank[:, x * QQ:(x + 1) * QQ], kv(kb, a)[0], T.qall[:, t * QB + a * QQ:t * QB + (a + 1) * QQ],
+                                True, True).then_inc(sem["sd%d" % t], 1)
+        g.vector.wait_ge(sem["sd%d" % t], 2 * HW)
+        g.vector.tensor_tensor(T.ssb[:, t * SW:(t + 1) * SW], bank[:, 0:SW], T.zero[:, 0:SW],
+                               AluOpType.max).then_inc(sem["rd%d" % t], 1)
 
-    def emit_o(chunk, c, base):
-        g.tensor.wait_ge(sem["rd%d" % c], 1)
-        for x, (wj, pj, rw) in enumerate(chunk):
-            g.tensor.matmul(T["op%d" % rw][:, 0:QQ], kv(wj, pj)[1], T.ssb[:, base + x * QQ:base + (x + 1) * QQ],
-                            nacc[rw] == 0, nacc[rw] == 2 * NC - 1).then_inc(sem["od%d" % rw], 1)
-            nacc[rw] += 1
+    def emit_o(t):
+        g.tensor.wait_ge(sem["rd%d" % t], 1)
+        if t >= NOP:
+            g.tensor.wait_ge(sem["oc%d" % (t - NOP)], 2 * HW)
+        bank = T["op%d" % (t % NOP)]
+        for a in range(HW):
+            for kb in (0, 1):
+                x = 2 * a + kb
+                g.tensor.matmul(bank[:, a * QQ:(a + 1) * QQ], kv(kb, a)[1], T.ssb[:, t * SW + x * QQ:t * SW + (x + 1) * QQ],
+                                kb == 0, kb == 1).then_inc(sem["od%d" % t], 1)
+        g.vector.wait_ge(sem["od%d" % t], 2 * HW)
+        for pp in (0, 1):
+            for a in range(HW):
+                if t == 0 and rank and pp == w:
+                    dst = T.yl[:, w * QS + a * QP:w * QS + (a + 1) * QP]
+                else:
+                    dst = T.osb[:, t * QB + pp * QS + a * QP:t * QB + pp * QS + (a + 1) * QP]
+                g.vector.tensor_copy(dst, bank[:, a * QQ + pp * QP:a * QQ + (pp + 1) * QP]).then_inc(sem["oc%d" % t], 1)
 
-    def copy_out(w, done):
-        g.vector.wait_ge(sem["od%d" % w], 2 * NC)
-        if PROC[w] == 0:
-            g.vector.tensor_copy(T.yl[:, head * QP:(head + 1) * QP],
-                                 T["op%d" % w][:, p * QP:(p + 1) * QP]).then_inc(sem.own, 1)
-            q = 1 - p
-            g.vector.tensor_copy(T.osb[:, w * QQ + q * QP:w * QQ + (q + 1) * QP],
-                                 T["op%d" % w][:, q * QP:(q + 1) * QP]).then_inc(done, 1)
-        else:
-            g.vector.tensor_copy(T.osb[:, w * QQ:(w + 1) * QQ], T["op%d" % w][:, 0:QQ]).then_inc(done, 1)
+    g.tensor.wait_ge(sem.pk, 2 * HW)
+    g.tensor.wait_ge(sem.kva, 2 * kne if rank else 4 * khe)
+    if rank:
+        g.tensor.wait_ge(sem.ldo, 32)
+    for t in range(NC):
+        emit_s(t)
+        if t:
+            emit_o(t - 1)
+    emit_o(NC - 1)
 
-    g.vector.wait_ge(sem.zf, 1)
-    for si, st in enumerate(STEPS):
-        t = min(si, NC - 1)
-        if t not in waited:
-            waited.append(t)
-            g.tensor.wait_ge(sem["arr%d" % t], narr[t])
-            if PROC[t] == 0:
-                g.tensor.wait_ge(sem.selfp, 1)
-                g.tensor.wait_ge(sem["ld%d" % n0], nld[n0])
-        prev = None
-        for chunk in st:
-            cur = (chunk,) + emit_s(chunk)
-            if prev:
-                emit_o(*prev)
-            prev = cur
-        emit_o(*prev)
-        if si == NC - 1:
-            for w in range(NC - 1):
-                copy_out(w, sem.oca)
-    copy_out(NC - 1, sem.ocb)
-
-    g.wait_ge(sem.oca, NC - 1)
-    nyarr = 0
-    if RETH:
-        rid, pid, _ = topo.addr(helper[core])
-        g.remote_dma(T.hob[:, 0:len(RETH) * QQ], T.osb[:, RETH[0] * QQ:(RETH[-1] + 1) * QQ], sem.hor, sem.sent, pid, rid,
-                     sum(stay))
-        sent += len(stay)
-        nyarr += 2 * len(RETH) * _split(off, 2 * len(RETH))[1]
-    trs, k = _ret(T, topo, mem, ci, p, [w for w in range(NC - 1) if w != w0 and w not in RETH], off, T.osb, 0)
-    sent += k * len(trs) + len(stay)
-    nyarr += k * len(trs) + len(stay)
-    trs.append(_tr(topo, mate_core, sum(stay), sem.yarr, T.osb[:, w0 * QQ + (1 - p) * QP:w0 * QQ + (2 - p) * QP],
-                   T.yl[:, head * QP:(head + 1) * QP]))
-    g.remote_dma_fused(trs, local_sem=sem.sent)
-    g.wait_ge(sem.ocb, 1)
-    trs, k = _ret(T, topo, mem, ci, p, [NC - 1], off, T.osb, 0)
-    g.remote_dma_fused(trs, local_sem=sem.sent)
-    sent += k * len(trs)
-    nyarr += k * len(trs)
+    nya = {}
+    for call in RCALLS:
+        for t in call:
+            g.wait_ge(sem["oc%d" % t], 2 * HW)
+        m, k = _split(stay if call == (0,) else off, 2 * len(call))
+        trs = []
+        for t in call:
+            nya[t] = (3 if t == 0 else 4) * k
+            for pp in (0, 1):
+                mask = m.pop(0)
+                dst_core = mem[(ci - t) % NC][pp]
+                if dst_core == core:
+                    continue
+                trs.append(_tr(topo, dst_core, mask, sem["ya%d" % t], T.osb[:, t * QB + pp * QS:t * QB + (pp + 1) * QS],
+                               T.yl[:, t * YW + w * QS:t * YW + (w + 1) * QS]))
+                sent += k
+        g.remote_dma_fused(trs, local_sem=sem.sent)
     g.wait_ge(sem.sent, sent)
+    if not rank:
+        return
 
-    g.sync.wait_ge(sem.yarr, nyarr)
-    g.sync.wait_ge(sem.own, 1)
-    g.sync.dma_start(T.y[:, :], T.yl[:, :]).then_inc(sem.stored, 16)
+    g.tensor.wait_ge(sem.idn, 1)
+    g.tensor.wait_ge(sem.oc0, 2 * HW)
+    for s in range(NC):
+        g.tensor.wait_ge(sem["ya%d" % s], nya[s])
+        g.tensor.matmul(T.ysum[:, 0:YW], T.ident[:, :], T.yl[:, s * YW:(s + 1) * YW], s == 0, s == NC - 1).then_inc(sem.ysd, 1)
+    g.vector.wait_ge(sem.ysd, NC)
+    g.vector.tensor_copy(T.yo[:, :], T.ysum[:, 0:YW]).then_inc(sem.yc, 1)
+    g.sync.wait_ge(sem.yc, 1)
+    g.sync.dma_start(T.y[:, :], T.yo[:, :]).then_inc(sem.stored, 16)
     g.sync.wait_ge(sem.stored, 16)

from concourse.bass import DstId, RemoteDMATransfer
from concourse.mybir import AluOpType

QP, KP = 32, 128
NC = 6
HW = 3
QQ = 2 * QP
QS = HW * QP
QB = 2 * QS
KS = HW * KP
YW = 12 * QP
SW = 2 * HW * QQ
QCALLS = ((1, 2), (3, 4), (5,))
RCALLS = ((0,), (1, 2), (3, 4), (5,))
NOP = 4

SCRATCH = {
    "qs": ("sbuf", [128, 12 * QP], "bfloat16"),
    "ks": ("sbuf", [128, 12 * KP], "bfloat16"),
    "vs": ("sbuf", [128, 12 * KP], "bfloat16"),
    "qraw": ("sbuf", [128, QB], "bfloat16"),
    "qall": ("sbuf", [128, NC * QB], "bfloat16"),
    "kl": ("sbuf", [128, 2 * KS], "bfloat16"),
    "vl": ("sbuf", [128, 2 * KS], "bfloat16"),
    "zero": ("sbuf", [128, SW], "float32"),
    "ones": ("sbuf", [128, 128], "bfloat16"),
    "ident": ("sbuf", [128, 128], "bfloat16"),
    "ssb": ("sbuf", [128, NC * SW], "bfloat16"),
    "osb": ("sbuf", [128, NC * QB], "bfloat16"),
    "yl": ("sbuf", [128, NC * YW], "bfloat16"),
    "yo": ("sbuf", [128, YW], "bfloat16"),
    "sp0": ("psum", [128, 512], "float32"),
    "sp1": ("psum", [128, 512], "float32"),
    "ysum": ("psum", [128, 512], "float32"),
}
for _w in range(NOP):
    SCRATCH["op%d" % _w] = ("psum", [128, 512], "float32")

SEMAPHORES = (["ldq", "ldh", "ldn", "ldo", "zf", "onesf", "idn", "qh", "pk", "kva", "sent", "ysd", "yc", "stored"]
              + ["arrq%d" % i for i in range(NC)] + ["ya%d" % i for i in range(NC)]
              + ["sd%d" % i for i in range(NC)] + ["rd%d" % i for i in range(NC)]
              + ["od%d" % i for i in range(NC)] + ["oc%d" % i for i in range(NC)])

_CACHE = {}


def _perms(lst):
    if len(lst) < 2:
        return [list(lst)]
    return [[x] + r for i, x in enumerate(lst) for r in _perms(lst[:i] + lst[i + 1:])]


def _plan(T, topo):
    if "p" in _CACHE:
        return _CACHE["p"]
    cores = list(T.cores)
    chips = sorted({topo.chip(c) for c in cores})
    every = range(max(chips) + 2)

    def way(a, b):
        if topo.same_plane(a, b):
            return [("out", a), ("in", b)]
        if topo.mates(a, b):
            return [("mate", a)]
        m = [x for x in every if topo.mates(a, x)][0]
        return [("mate", a), ("out", m), ("in", b)]

    best = None
    for rest in _perms(chips[1:]):
        ring = [chips[0]] + rest
        by_step = 0
        sq = 0
        for s in range(1, NC):
            now = {}
            for i, a in enumerate(ring):
                for l in way(a, ring[(i + s) % NC]):
                    now[l] = now.get(l, 0) + 1
            by_step += max(now.values())
            sq += sum(v * v for v in now.values())
        score = (by_step, sq)
        if best is None or score < best[0]:
            best = (score, ring)
    ring = best[1]
    mem = [sorted(c for c in cores if topo.chip(c) == ch) for ch in ring]
    work = []
    for two in mem:
        cand = [x for x in range(max(cores) + 1)
                if topo.chip(x) == topo.chip(two[0]) and x not in cores and topo.die(x) != topo.die(two[0])
                and all(topo.may_write(x, d) for d in cores)]
        work.append(list(two) + cand[:2])
    _CACHE["p"] = (mem, work)
    return _CACHE["p"]


def _bits(m):
    return [1 << e for e in range(m.bit_length()) if (m >> e) & 1]


def _split(bits, n):
    k = 1
    while 2 * k * n <= len(bits):
        k *= 2
    return [sum(bits[i * k:(i + 1) * k]) for i in range(n)], k


def _tr(topo, dst_core, mask, sem, src, dst):
    rid, pid, _ = topo.addr(dst_core)
    return RemoteDMATransfer(dst_ids=[DstId(rid=rid, pnc=pid)], dma_engine_mask=mask, remote_sem=sem, src=src, dst=dst)


def rank_program(g, core, T, topo):
    mem, work = _plan(T, topo)
    here = [(i, four.index(core)) for i, four in enumerate(work) if core in four]
    if not here:
        return
    ci, w = here[0]
    rank = w < 2
    sem = T.sem
    off = _bits(topo.mask(core, work[(ci + 1) % NC][w]))
    stay = [b for b in _bits(topo.mask(core, work[ci][(w + 1) % 4])) if b not in off]
    qhe = _split(off, 3)[1]
    khe = _split(stay, 4)[1]
    kne = _split(stay, 2)[1]
    sent = 0

    if rank:
        g.sync.dma_start(T.qs[:, :], T.q[:, :]).then_inc(sem.ldq, 16)
        for a, b, s in ((2 * KS, 4 * KS, sem.ldh), ((1 - w) * KS, (2 - w) * KS, sem.ldn), (w * KS, (w + 1) * KS, sem.ldo)):
            g.sync.dma_start(T.ks[:, a:b], T.k[:, a:b]).then_inc(s, 16)
            g.scalar.dma_start(T.vs[:, a:b], T.v[:, a:b]).then_inc(s, 16)

    g.vector.memset(T.zero[:, :], 0.0).then_inc(sem.zf, 1)
    if rank:
        g.vector.memset(T.ones[:, :], 1.0).then_inc(sem.onesf, 1)
        g.vector.wait_ge(sem.ldq, 16)
    g.vector.wait_ge(sem.qh, qhe * (1 if rank else 2))
    for a in range(HW):
        for pp in (0, 1):
            if rank and pp == w:
                src = T.qs[:, (w * HW + a) * QP:(w * HW + a + 1) * QP]
            else:
                src = T.qraw[:, pp * QS + a * QP:pp * QS + (a + 1) * QP]
            g.vector.tensor_copy(T.qall[:, a * QQ + pp * QP:a * QQ + (pp + 1) * QP], src).then_inc(sem.pk, 1)
    g.vector.wait_ge(sem.zf, 1)

    if rank:
        g.wait_ge(sem.onesf, 1)
        g.affine_select(T.ident[:, :], T.ones[:, :], [[-1, 128]], AluOpType.is_equal, 0.0, 0, 1).then_inc(sem.idn, 1)
        g.wait_ge(sem.ldq, 16)
        m, k = _split(off, 3)
        g.remote_dma_fused([_tr(topo, work[ci][x], m[i], sem.qh, T.qs[:, x * QS:(x + 1) * QS], T.qraw[:, w * QS:(w + 1) * QS])
                            for i, x in enumerate(y for y in range(4) if y != w)], local_sem=sem.sent)
        sent += 3 * k
        g.wait_ge(sem.ldh, 32)
        m, k = _split(stay, 4)
        trs = []
        for x in (2, 3):
            for src, dst in ((T.ks, T.kl), (T.vs, T.vl)):
                trs.append(_tr(topo, work[ci][x], m.pop(0), sem.kva, src[:, x * KS:(x + 1) * KS], dst[:, w * KS:(w + 1) * KS]))
        g.remote_dma_fused(trs, local_sem=sem.sent)
        sent += 4 * k
        g.wait_ge(sem.ldn, 32)
        m, k = _split(stay, 2)
        x = 1 - w
        g.remote_dma_fused([_tr(topo, work[ci][x], m[i], sem.kva, src[:, x * KS:(x + 1) * KS], dst[:, w * KS:(w + 1) * KS])
                            for i, (src, dst) in enumerate(((T.ks, T.kl), (T.vs, T.vl)))], local_sem=sem.sent)
        sent += 2 * k

    narr = {}
    g.wait_ge(sem.pk, 2 * HW)
    for call in QCALLS:
        m, k = _split(off, len(call))
        g.remote_dma_fused([_tr(topo, work[(ci + s) % NC][w], m[i], sem["arrq%d" % s], T.qall[:, 0:QB],
                                T.qall[:, s * QB:(s + 1) * QB]) for i, s in enumerate(call)], local_sem=sem.sent)
        sent += k * len(call)
        for s in call:
            narr[s] = k

    sp = [T.sp0, T.sp1]

    def kv(kb, a):
        if rank and kb == w:
            c = (w * HW + a) * KP
            return T.ks[:, c:c + KP], T.vs[:, c:c + KP]
        c = kb * KS + a * KP
        return T.kl[:, c:c + KP], T.vl[:, c:c + KP]

    def emit_s(t):
        if t:
            g.tensor.wait_ge(sem["arrq%d" % t], narr[t])
        bank = sp[t % 2]
        for a in range(HW):
            for kb in (0, 1):
                x = 2 * a + kb
                g.tensor.matmul(bank[:, x * QQ:(x + 1) * QQ], kv(kb, a)[0], T.qall[:, t * QB + a * QQ:t * QB + (a + 1) * QQ],
                                True, True).then_inc(sem["sd%d" % t], 1)
        g.vector.wait_ge(sem["sd%d" % t], 2 * HW)
        g.vector.tensor_tensor(T.ssb[:, t * SW:(t + 1) * SW], bank[:, 0:SW], T.zero[:, 0:SW],
                               AluOpType.max).then_inc(sem["rd%d" % t], 1)

    def emit_o(t):
        g.tensor.wait_ge(sem["rd%d" % t], 1)
        if t >= NOP:
            g.tensor.wait_ge(sem["oc%d" % (t - NOP)], 2 * HW)
        bank = T["op%d" % (t % NOP)]
        for a in range(HW):
            for kb in (0, 1):
                x = 2 * a + kb
                g.tensor.matmul(bank[:, a * QQ:(a + 1) * QQ], kv(kb, a)[1], T.ssb[:, t * SW + x * QQ:t * SW + (x + 1) * QQ],
                                kb == 0, kb == 1).then_inc(sem["od%d" % t], 1)
        g.vector.wait_ge(sem["od%d" % t], 2 * HW)
        for pp in (0, 1):
            for a in range(HW):
                if t == 0 and rank and pp == w:
                    dst = T.yl[:, w * QS + a * QP:w * QS + (a + 1) * QP]
                else:
                    dst = T.osb[:, t * QB + pp * QS + a * QP:t * QB + pp * QS + (a + 1) * QP]
                g.vector.tensor_copy(dst, bank[:, a * QQ + pp * QP:a * QQ + (pp + 1) * QP]).then_inc(sem["oc%d" % t], 1)

    g.tensor.wait_ge(sem.pk, 2 * HW)
    g.tensor.wait_ge(sem.kva, 2 * kne if rank else 4 * khe)
    if rank:
        g.tensor.wait_ge(sem.ldo, 32)
    for t in range(NC):
        emit_s(t)
        if t:
            emit_o(t - 1)
    emit_o(NC - 1)

    nya = {}
    for call in RCALLS:
        for t in call:
            g.wait_ge(sem["oc%d" % t], 2 * HW)
        m, k = _split(stay if call == (0,) else off, 2 * len(call))
        trs = []
        for t in call:
            nya[t] = (3 if t == 0 else 4) * k
            for pp in (0, 1):
                mask = m.pop(0)
                dst_core = mem[(ci - t) % NC][pp]
                if dst_core == core:
                    continue
                trs.append(_tr(topo, dst_core, mask, sem["ya%d" % t], T.osb[:, t * QB + pp * QS:t * QB + (pp + 1) * QS],
                               T.yl[:, t * YW + w * QS:t * YW + (w + 1) * QS]))
                sent += k
        g.remote_dma_fused(trs, local_sem=sem.sent)
    g.wait_ge(sem.sent, sent)
    if not rank:
        return

    g.tensor.wait_ge(sem.idn, 1)
    g.tensor.wait_ge(sem.oc0, 2 * HW)
    for s in range(NC):
        g.tensor.wait_ge(sem["ya%d" % s], nya[s])
        g.tensor.matmul(T.ysum[:, 0:YW], T.ident[:, :], T.yl[:, s * YW:(s + 1) * YW], s == 0, s == NC - 1).then_inc(sem.ysd, 1)
    g.vector.wait_ge(sem.ysd, NC)
    g.vector.tensor_copy(T.yo[:, :], T.ysum[:, 0:YW]).then_inc(sem.yc, 1)
    g.sync.wait_ge(sem.yc, 1)
    g.sync.dma_start(T.y[:, :], T.yo[:, :]).then_inc(sem.stored, 16)
    g.sync.wait_ge(sem.stored, 16)
